import numpy as np
import ml_dtypes


def mxq(x, axis, fmt="e4m3"):
    dtype, down = {"e4m3": (ml_dtypes.float8_e4m3fn, 7), "e5m2": (ml_dtypes.float8_e5m2, 14)}[fmt]
    v = np.moveaxis(np.asarray(x, np.float32).astype(ml_dtypes.bfloat16).astype(np.float64), axis, -1)
    blocks = v.reshape(v.shape[:-1] + (-1, 32))
    amax = np.abs(blocks).max(-1, keepdims=True)
    byte = np.maximum(np.where(amax > 0, np.frexp(amax)[1] - 1 + 127, 0) - down, 1)
    scale = np.exp2(byte - 127.0)
    codes = (blocks / scale).astype(np.float32).astype(dtype).astype(np.float64)
    return np.moveaxis((codes * scale).reshape(v.shape), -1, axis)


WIDE = False


def mx_kscale(k):
    if not WIDE:
        return np.ones(k)
    levels = np.array([10, -10, 5, -5, 0])
    if k % 512:
        return np.exp2(np.random.permutation(np.resize(levels, k // 32))).repeat(32)
    a = np.empty((k // 512, 16))
    for p in range(k // 512):
        a[p, :8] = np.random.permutation(np.resize(levels, 8))
        for g in range(8):
            far = levels[np.abs(levels - a[p, g]) >= 10]
            a[p, g + 8] = far[np.random.randint(len(far))]
    return np.exp2(a.ravel()).repeat(32)


def f64(x):
    return np.asarray(x).astype(np.float64)


def striped(idx):
    return np.tile(idx.reshape(-1, 16).T, (8, 1)).astype(np.uint16)


def unstriped(offs):
    return offs[:16].T.reshape(-1).astype(np.int64)


def striped8(idx):
    return np.concatenate([x.reshape(-1, 16).T for x in idx]).astype(np.uint16)


def runs(offs, k):
    lists = np.stack([offs[16 * r : 16 * r + 16].T.reshape(-1) for r in range(8)]).astype(np.int64)
    return lists[np.arange(k) % 512 // 64]


def pack_weight(w):
    k, n = w.shape
    w = f64(np.asarray(w, np.float32).astype(ml_dtypes.bfloat16)).reshape(k // 32, 32, n)
    amax = np.abs(w).max(1)
    byte = np.clip(np.where(amax > 0, np.frexp(amax)[1] - 1 + 127 - 7, 1), 1, 254)
    scaled = (w * np.exp2(127.0 - byte)[:, None, :]).reshape(k, n).astype(np.float32)
    words = np.ascontiguousarray(scaled.reshape(k // 512, 128, 4, n).transpose(0, 1, 3, 2)).astype(ml_dtypes.float8_e4m3fn).view(np.uint8)
    return words, np.ascontiguousarray(byte.astype(np.uint8).reshape(k // 512, 16, n))


def unpack_weight(words, scales):
    g, p, n, _ = words.shape
    vals = np.ascontiguousarray(words).view(ml_dtypes.float8_e4m3fn).astype(np.float64) * np.repeat(np.exp2(scales.astype(np.float64) - 127.0), 8, axis=1)[..., None]
    return vals.transpose(0, 1, 3, 2).reshape(g * 512, n)

def planes(y):
    n, m = y.shape
    v = y.astype(np.float32).astype(ml_dtypes.bfloat16).astype(np.float64).reshape(n // 32, 32, m)
    top = np.abs(v).max(1)
    byte = np.clip(np.where(top > 0, np.frexp(top)[1] - 1 + 127 - 7, 1), 1, 254)
    codes = (v * np.exp2(127.0 - byte)[:, None, :]).reshape(n, m).astype(np.float32).astype(ml_dtypes.float8_e4m3fn).view(np.uint8)
    words = codes.reshape(n // 512, 128, 4, m).transpose(0, 1, 3, 2)
    return np.ascontiguousarray(words), np.ascontiguousarray(byte.astype(np.uint8).reshape(n // 512, 16, m))


K, T, S, H, C = 512, 2048, 512, 512, 512


def setup_inputs():
    n = np.random.standard_normal
    s = mx_kscale(K)[:, None]
    packed_xT = pack_weight(n((K, T)) * s)
    packed_w1 = pack_weight(n((K, H)) / np.sqrt(K) / s)
    return {
        "x_words": packed_xT[0],
        "x_scales": packed_xT[1],
        "w1_words": packed_w1[0],
        "w1_scales": packed_w1[1],
        "gs": (np.random.uniform(0.5, 1.5, (K, 1)) / s).astype(np.float32),
        "wb": (n((K, S)) / np.sqrt(K) / s).astype(np.float32),
        "offs": striped(np.random.permutation(T)[:S]),
        "n1": striped(np.random.permutation(S)),
        "n2": striped(np.random.permutation(S)),
        "cand": striped(np.random.permutation(T)[:C]),
        "cb": striped(np.random.permutation(T)[:C]),
        "n3": striped8(np.stack([np.random.permutation(S) for _ in range(8)])),
        "n4": striped8(np.stack([np.random.permutation(S) for _ in range(8)])),
        "n5": striped8(np.stack([np.random.permutation(S) for _ in range(8)])),
        "n6": striped8(np.stack([np.random.permutation(S) for _ in range(8)])),
    }


def reference(x_words, x_scales, w1_words, w1_scales, gs, wb, offs, n1, n2, cand, cb, n3, n4, n5, n6):
    x_cand = unpack_weight(x_words, x_scales)[:, unstriped(cand)]
    xq = unpack_weight(x_words, x_scales)[:, unstriped(offs)]
    y = unpack_weight(w1_words, w1_scales).T @ xq
    pa = y[:, unstriped(n1)]
    pb = y[:, unstriped(n2)]
    z = f64(gs) * (np.maximum(np.minimum(y, pa), np.minimum(np.maximum(y, pa), pb)))
    a = 0.0625 * ((x_cand.T @ mxq(z, 0, "e4m3")))
    x_cb = unpack_weight(x_words, x_scales)[:, unstriped(cb)]
    b = x_cb.T @ mxq(f64(wb), 0, "e4m3")
    out_0 = np.maximum(a[np.arange(C)[:, None], runs(n3, C)] + b[np.arange(C)[:, None], runs(n5, C)], a[np.arange(C)[:, None], runs(n4, C)] + b[np.arange(C)[:, None], runs(n6, C)])
    return (out_0,) + planes(out_0)

@@ -1,0 +1,210 @@
+from contextlib import ExitStack
+
+import concourse.mybir as mybir
+
+F32 = mybir.dt.float32
+BF16 = mybir.dt.bfloat16
+I32 = mybir.dt.int32
+U32 = mybir.dt.uint32
+U16 = mybir.dt.uint16
+U8 = mybir.dt.uint8
+FP8X4 = mybir.dt.float8_e4m3fn_x4
+ALU = mybir.AluOpType
+COPY = mybir.ActivationFunctionType.Copy
+
+P = 128
+PACK = 4
+T = 2048
+S = 512
+HALF = S // 2
+CHUNKS = ((0, 256), (256, 128), (384, 128))
+
+FLOPS = 3 * 2 * 512 * 512 * 512
+
+
+def tile_picked_cdswpathbmed_none_po_kernel(
+    tc, x_words, x_scales, w1_words, w1_scales, gs, wb, offs, n1, n2, cand, cb, n3, n4, n5, n6, out_0, out_1, out_2
+):
+    nc = tc.nc
+
+    with ExitStack() as ctx:
+        keep = ctx.enter_context(tc.tile_pool(name="keep", bufs=1))
+        psum = ctx.enter_context(tc.psum_pool(name="psum", bufs=1))
+
+        def sb(name, shape, dtype, tag=None):
+            return keep.tile(shape, dtype, name=name, tag=tag or name, align_bytes=64)
+
+        def load_list(name, src):
+            t = keep.tile([P, S // 16], U16, name=name)
+            nc.sync.dma_start(t[:], src)
+            return t
+
+        def entries(lst, first, count):
+            return lst[:, first // 16 : (first + count) // 16]
+
+        def load_scale_rows(queue, dst, src):
+            for q in range(4):
+                queue.dma_start(dst[32 * q : 32 * q + 4, :].bitcast(I32), src[0, 4 * q : 4 * q + 4, :].bitcast(I32))
+
+        def words_view(src):
+            return src[0].rearrange("p n t -> p (n t)")
+
+        def interleave(move, dst, src):
+            move(out=dst.rearrange("p (c i) t -> p c t i", i=4), in_=src.rearrange("p t (c i) -> p c t i", i=4))
+
+        def quantize(codes, scales, grouped):
+            nc.vector.quantize_mx(out=codes.bitcast(FP8X4), scales=scales, in_=grouped.rearrange("p n t -> p (n t)"))
+
+        def product(dst, st_codes, st_scales, mv_codes, mv_scales):
+            nc.tensor.matmul_mx(
+                out=dst,
+                lhsT=st_codes.bitcast(FP8X4),
+                lhsT_scale=st_scales,
+                rhs=mv_codes.bitcast(FP8X4),
+                rhs_scale=mv_scales,
+                start=True,
+                stop=True,
+            )
+
+        x_sc = sb("x_sc", [P, T], U8)
+        w1_sc = sb("w1_sc", [P, S], U8)
+        nc.gpsimd.memset(w1_sc[:].bitcast(I32), 0)
+
+        l_offs = load_list("l_offs", offs)
+        for q in range(4):
+            rows = x_scales[0, 4 * q : 4 * q + 4, :].bitcast(I32)
+            nc.sync.dma_start(x_sc[32 * q : 32 * q + 32, :].bitcast(I32), rows.unsqueeze(0).broadcast_to([8, 4, T // 4]))
+        w1_w = sb("w1_w", [P, S], U32)
+        nc.sync.dma_start(w1_w[:].bitcast(I32), words_view(w1_words).bitcast(I32))
+        l_cand = load_list("l_cand", cand)
+        x_w = sb("x_w", [P, T], U32)
+        nc.sync.dma_start(x_w[:].bitcast(I32), words_view(x_words).bitcast(I32))
+        load_scale_rows(nc.sync, w1_sc, w1_scales)
+        gain = sb("gain", [P, PACK], F32)
+        nc.gpsimd.dma_start(gain[:], gs.rearrange("(p t) o -> p (t o)", t=PACK))
+        l_cb = load_list("l_cb", cb)
+        l_n1 = load_list("l_n1", n1)
+        l_n2 = load_list("l_n2", n2)
+        wb_raw = sb("wb_raw", [P, PACK, S], F32)
+        nc.sync.dma_start(wb_raw[:], wb.rearrange("(p t) n -> p t n", t=PACK))
+        l_n5 = load_list("l_n5", n5)
+        l_n6 = load_list("l_n6", n6)
+        l_n3 = load_list("l_n3", n3)
+        l_n4 = load_list("l_n4", n4)
+
+        q_sc = sb("q_sc", [P, S], U8)
+        nc.vector.tensor_copy(out=q_sc[:], in_=x_sc[:].indirect(l_offs[:]))
+        w1_wd = sb("w1_wd", [P, PACK, P], U32)
+        nc.vector.tensor_copy(out=w1_wd[:], in_=w1_w[:].rearrange("p (m t) -> p t m", t=PACK))
+        picked_sc = sb("picked_sc", [P, 2, S], U8)
+        nc.vector.tensor_copy(out=picked_sc[:, 0, :], in_=x_sc[:].indirect(l_cand[:]))
+        w1_sd = sb("w1_sd", [P, PACK, P], U8)
+
+        q_w = [sb(f"q_w{h}", [P, HALF], U32) for h in range(2)]
+        y_win = [sb(f"y_win{t}", [P, S], F32) for t in range(PACK)]
+        for h in range(2):
+            cols = slice(h * HALF, (h + 1) * HALF)
+            nc.vector.tensor_copy(out=q_w[h][:], in_=x_w[:].indirect(entries(l_offs, h * HALF, HALF)))
+            if h == 0:
+                nc.vector.tensor_copy(out=w1_sd[:], in_=w1_sc[:].rearrange("p (m t) -> p t m", t=PACK))
+            for u in range(2):
+                bank = psum.tile([P, 2, HALF], F32, name=f"bank{2 * h + u}")
+                for e in range(2):
+                    t = 2 * u + e
+                    product(bank[:, e, :], w1_wd[:, t, :], w1_sd[:, t, :], q_w[h][:], q_sc[:, cols])
+                for e in range(2):
+                    t = 2 * u + e
+                    nc.scalar.activation(out=y_win[t][:, cols], in_=bank[:, e, :], func=COPY, scale=gain[:, t : t + 1])
+
+        cb_w = sb("cb_w", [P, PACK, P], U32)
+        nc.vector.tensor_copy(out=picked_sc[:, 1, :], in_=x_sc[:].indirect(l_cb[:]))
+        nc.vector.tensor_copy(out=cb_w[:].rearrange("p t m -> p m t"), in_=x_w[:].indirect(l_cb[:]))
+        dealt_sc = sb("dealt_sc", [P, 2, PACK, P], U8)
+        nc.vector.tensor_copy(out=dealt_sc[:], in_=picked_sc[:].rearrange("p l (m t) -> p l t m", t=PACK))
+
+        cand_w = sb("cand_w", [P, PACK, P], U32, tag="w1_sc")
+        nc.vector.tensor_copy(out=cand_w[:].rearrange("p t m -> p m t"), in_=x_w[:].indirect(l_cand[:]))
+        wb_grouped = sb("wb_grouped", [P, S, PACK], BF16)
+        interleave(nc.vector.tensor_copy, wb_grouped[:], wb_raw[:])
+
+        a_bank = [psum.tile([P, S], F32, name=f"bank{t}") for t in range(PACK)]
+        b_bank = [psum.tile([P, S], F32, name=f"bank{4 + t}") for t in range(PACK)]
+        b_win = [sb(f"b_win{t}", [P, S], F32) for t in range(PACK)]
+        a_win = [sb(f"a_win{t}", [P, S], F32) for t in range(PACK)]
+        for c, (first, width) in enumerate(CHUNKS):
+            cols = slice(first, first + width)
+            pa = sb(f"pa{c}", [P, PACK, width], BF16)
+            pb = sb(f"pb{c}", [P, PACK, width], BF16)
+            lo = sb(f"lo{c}", [P, PACK, width], BF16)
+            hi = sb(f"hi{c}", [P, PACK, width], BF16)
+            for t in range(PACK):
+                nc.scalar.activation(out=pa[:, t, :], in_=y_win[t][:].indirect(entries(l_n1, first, width)), func=COPY)
+                nc.scalar.activation(out=pb[:, t, :], in_=y_win[t][:].indirect(entries(l_n2, first, width)), func=COPY)
+            for u in range(2):
+                pair = slice(2 * u, 2 * u + 2)
+                nc.vector.tensor_tensor(out=hi[:, pair, :], in0=pa[:, pair, :], in1=pb[:, pair, :], op=ALU.max)
+                nc.vector.tensor_tensor(out=lo[:, pair, :], in0=pa[:, pair, :], in1=pb[:, pair, :], op=ALU.min)
+                for t in range(2 * u, 2 * u + 2):
+                    nc.vector.tensor_tensor(out=pa[:, t, :], in0=y_win[t][:, cols], in1=hi[:, t, :], op=ALU.min)
+                nc.vector.tensor_tensor(out=pb[:, pair, :], in0=pa[:, pair, :], in1=lo[:, pair, :], op=ALU.max)
+                if c == 0 and u == 0:
+                    wb_w = sb("wb_w", [P, S], U32)
+                    wb_sc = sb("wb_sc", [P, S], U8)
+                    quantize(wb_w[:], wb_sc[:], wb_grouped[:])
+                    for t in range(PACK):
+                        product(b_bank[t][:], cb_w[:, t, :], dealt_sc[:, 1, t, :], wb_w[:], wb_sc[:])
+            z_grouped = sb(f"z_grouped{c}", [P, width, PACK], BF16)
+            z_w = sb(f"z_w{c}", [P, width], U32)
+            z_sc = sb(f"z_sc{c}", [P, width], U8)
+            interleave(nc.vector.tensor_copy, z_grouped[:], pb[:])
+            quantize(z_w[:], z_sc[:], z_grouped[:])
+            for t in range(PACK):
+                product(a_bank[t][:, cols], cand_w[:, t, :], dealt_sc[:, 0, t, :], z_w[:], z_sc[:])
+        for t in range(PACK):
+            nc.scalar.copy(out=b_win[t][:], in_=b_bank[t][:])
+        for t in range(PACK):
+            if t < 2:
+                nc.vector.tensor_scalar_mul(a_win[t][:], a_bank[t][:], 0.0625)
+            else:
+                nc.scalar.activation(out=a_win[t][:], in_=a_bank[t][:], func=COPY, scale=0.0625)
+
+        out_rows = out_0.rearrange("(p t) n -> p t n", t=PACK)
+        out_sc = sb("out_sc", [P, S], U8)
+        early = 2 * 2 * CHUNKS[0][1]
+        b_early = sb("b_early", [P, early], F32)
+        b_late = sb("b_late", [P, 2 * PACK * S - early], F32, tag=f"z_w{len(CHUNKS) - 1}")
+        b_near = {}
+        place = 0
+        for c, (first, width) in enumerate(CHUNKS):
+            for t in range(PACK):
+                for k, lst in enumerate((l_n5, l_n6)):
+                    if place < early:
+                        b_near[c, t, k] = b_early[:, place : place + width]
+                    else:
+                        b_near[c, t, k] = b_late[:, place - early : place - early + width]
+                    place += width
+                    nc.scalar.activation(out=b_near[c, t, k], in_=b_win[t][:].indirect(entries(lst, first, width)), func=COPY)
+        for c, (first, width) in enumerate(CHUNKS):
+            cols = slice(first, first + width)
+            sums = sb(f"sums{c}", [P, 2, PACK, width], F32)
+            res = sb(f"res{c}", [P, PACK, width], F32)
+            for t in range(PACK):
+                for k, lst in enumerate((l_n3, l_n4)):
+                    nc.vector.tensor_tensor(
+                        out=sums[:, k, t, :],
+                        in0=a_win[t][:].indirect(entries(lst, first, width)),
+                        in1=b_near[c, t, k],
+                        op=ALU.add,
+                    )
+            nc.vector.tensor_tensor(out=res[:], in0=sums[:, 0, :, :], in1=sums[:, 1, :, :], op=ALU.max)
+            nc.sync.dma_start(out_rows[:, :, cols], res[:])
+            res_grouped = sb(f"res_grouped{c}", [P, width, PACK], BF16)
+            interleave(nc.vector.tensor_copy if c == len(CHUNKS) - 1 else nc.scalar.copy, res_grouped[:], res[:])
+            out_w = sb(f"out_w{c}", [P, width], U32)
+            quantize(out_w[:], out_sc[:, cols], res_grouped[:])
+            nc.sync.dma_start(
+                words_view(out_1)[:, PACK * first : PACK * (first + width)].bitcast(I32), out_w[:].bitcast(I32)
+            )
+        for q in range(4):
+            queue = nc.sync if q % 2 else nc.scalar
+            queue.dma_start(out_2[0, 4 * q : 4 * q + 4, :].bitcast(I32), out_sc[32 * q : 32 * q + 4, :].bitcast(I32))

@@ -69,19 +69,25 @@ def tile_picked_cdswpathbmed_none_po_kernel(
         x_sc = sb("x_sc", [P, T], U8)
         w1_sc = sb("w1_sc", [P, S], U8)
         nc.gpsimd.memset(w1_sc[:].bitcast(I32), 0)
+        ya_win = [sb(f"ya_win{t}", [P, 2 * S if t < PACK - 1 else S], F32) for t in range(PACK)]
+        b_win = [sb(f"b_win{t}", [P, 2 * S], F32) for t in range(PACK)]
+        for win in ya_win[: PACK - 1] + b_win[:1]:
+            nc.vector.memset(win[:, S:].bitcast(I32), 0)
 
         l_offs = load_list("l_offs", offs)
         for q in range(4):
             rows = x_scales[0, 4 * q : 4 * q + 4, :].bitcast(I32)
             nc.sync.dma_start(x_sc[32 * q : 32 * q + 32, :].bitcast(I32), rows.unsqueeze(0).broadcast_to([8, 4, T // 4]))
-        w1_w = sb("w1_w", [P, S], U32)
-        nc.sync.dma_start(w1_w[:].bitcast(I32), words_view(w1_words).bitcast(I32))
         l_cand = load_list("l_cand", cand)
         x_w = sb("x_w", [P, T], U32)
         nc.sync.dma_start(x_w[:].bitcast(I32), words_view(x_words).bitcast(I32))
+        w1_w = sb("w1_w", [P, S], U32)
+        nc.sync.dma_start(w1_w[:].bitcast(I32), words_view(w1_words).bitcast(I32))
         load_scale_rows(nc.sync, w1_sc, w1_scales)
         gain = sb("gain", [P, PACK], F32)
         nc.gpsimd.dma_start(gain[:], gs.rearrange("(p t) o -> p (t o)", t=PACK))
+        for win in b_win[1:]:
+            nc.gpsimd.memset(win[:, S:].bitcast(I32), 0)
         l_cb = load_list("l_cb", cb)
         l_n1 = load_list("l_n1", n1)
         l_n2 = load_list("l_n2", n2)
@@ -95,17 +101,16 @@ def tile_picked_cdswpathbmed_none_po_kernel(
         q_sc = sb("q_sc", [P, S], U8)
         nc.vector.tensor_copy(out=q_sc[:], in_=x_sc[:].indirect(l_offs[:]))
         w1_wd = sb("w1_wd", [P, PACK, P], U32)
-        nc.vector.tensor_copy(out=w1_wd[:], in_=w1_w[:].rearrange("p (m t) -> p t m", t=PACK))
         picked_sc = sb("picked_sc", [P, 2, S], U8)
         nc.vector.tensor_copy(out=picked_sc[:, 0, :], in_=x_sc[:].indirect(l_cand[:]))
         w1_sd = sb("w1_sd", [P, PACK, P], U8)
 
-        q_w = [sb(f"q_w{h}", [P, HALF], U32) for h in range(2)]
-        y_win = [sb(f"y_win{t}", [P, S], F32) for t in range(PACK)]
+        q_w = [sb("q_w0", [P, HALF], U32), sb("q_w1", [P, HALF], U32, tag="w1_sc")]
         for h in range(2):
             cols = slice(h * HALF, (h + 1) * HALF)
             nc.vector.tensor_copy(out=q_w[h][:], in_=x_w[:].indirect(entries(l_offs, h * HALF, HALF)))
             if h == 0:
+                nc.vector.tensor_copy(out=w1_wd[:], in_=w1_w[:].rearrange("p (m t) -> p t m", t=PACK))
                 nc.vector.tensor_copy(out=w1_sd[:], in_=w1_sc[:].rearrange("p (m t) -> p t m", t=PACK))
             for u in range(2):
                 bank = psum.tile([P, 2, HALF], F32, name=f"bank{2 * h + u}")
@@ -114,7 +119,7 @@ def tile_picked_cdswpathbmed_none_po_kernel(
                     product(bank[:, e, :], w1_wd[:, t, :], w1_sd[:, t, :], q_w[h][:], q_sc[:, cols])
                 for e in range(2):
                     t = 2 * u + e
-                    nc.scalar.activation(out=y_win[t][:, cols], in_=bank[:, e, :], func=COPY, scale=gain[:, t : t + 1])
+                    nc.scalar.activation(out=ya_win[t][:, cols], in_=bank[:, e, :], func=COPY, scale=gain[:, t : t + 1])
 
         cb_w = sb("cb_w", [P, PACK, P], U32)
         nc.vector.tensor_copy(out=picked_sc[:, 1, :], in_=x_sc[:].indirect(l_cb[:]))
@@ -127,79 +132,84 @@ def tile_picked_cdswpathbmed_none_po_kernel(
         wb_grouped = sb("wb_grouped", [P, S, PACK], BF16)
         interleave(nc.vector.tensor_copy, wb_grouped[:], wb_raw[:])
 
-        a_bank = [psum.tile([P, S], F32, name=f"bank{t}") for t in range(PACK)]
+        wb_w = sb("wb_w", [P, S], U32)
+        wb_sc = sb("wb_sc", [P, S], U8)
+        quantize(wb_w[:], wb_sc[:], wb_grouped[:])
         b_bank = [psum.tile([P, S], F32, name=f"bank{4 + t}") for t in range(PACK)]
-        b_win = [sb(f"b_win{t}", [P, S], F32) for t in range(PACK)]
-        a_win = [sb(f"a_win{t}", [P, S], F32) for t in range(PACK)]
-        for c, (first, width) in enumerate(CHUNKS):
+        for t in range(PACK):
+            product(b_bank[t][:], cb_w[:, t, :], dealt_sc[:, 1, t, :], wb_w[:], wb_sc[:])
+
+        pa = sb("pa", [P, PACK, S], BF16)
+        pb = sb("pb", [P, PACK, S], BF16)
+        lo = sb("lo", [P, PACK, S], BF16)
+        hi = sb("hi", [P, PACK, S], BF16)
+        z_planes = sb("z_planes", [P, PACK, S], BF16)
+
+        def median(t, first, width):
             cols = slice(first, first + width)
-            pa = sb(f"pa{c}", [P, PACK, width], BF16)
-            pb = sb(f"pb{c}", [P, PACK, width], BF16)
-            lo = sb(f"lo{c}", [P, PACK, width], BF16)
-            hi = sb(f"hi{c}", [P, PACK, width], BF16)
-            for t in range(PACK):
-                nc.scalar.activation(out=pa[:, t, :], in_=y_win[t][:].indirect(entries(l_n1, first, width)), func=COPY)
-                nc.scalar.activation(out=pb[:, t, :], in_=y_win[t][:].indirect(entries(l_n2, first, width)), func=COPY)
-            for u in range(2):
-                pair = slice(2 * u, 2 * u + 2)
-                nc.vector.tensor_tensor(out=hi[:, pair, :], in0=pa[:, pair, :], in1=pb[:, pair, :], op=ALU.max)
-                nc.vector.tensor_tensor(out=lo[:, pair, :], in0=pa[:, pair, :], in1=pb[:, pair, :], op=ALU.min)
-                for t in range(2 * u, 2 * u + 2):
-                    nc.vector.tensor_tensor(out=pa[:, t, :], in0=y_win[t][:, cols], in1=hi[:, t, :], op=ALU.min)
-                nc.vector.tensor_tensor(out=pb[:, pair, :], in0=pa[:, pair, :], in1=lo[:, pair, :], op=ALU.max)
-                if c == 0 and u == 0:
-                    wb_w = sb("wb_w", [P, S], U32)
-                    wb_sc = sb("wb_sc", [P, S], U8)
-                    quantize(wb_w[:], wb_sc[:], wb_grouped[:])
-                    for t in range(PACK):
-                        product(b_bank[t][:], cb_w[:, t, :], dealt_sc[:, 1, t, :], wb_w[:], wb_sc[:])
+            nc.scalar.activation(out=pa[:, t, cols], in_=ya_win[t][:].indirect(entries(l_n1, first, width)), func=COPY)
+            nc.scalar.activation(out=pb[:, t, cols], in_=ya_win[t][:].indirect(entries(l_n2, first, width)), func=COPY)
+            nc.vector.tensor_tensor(out=hi[:, t, cols], in0=pa[:, t, cols], in1=pb[:, t, cols], op=ALU.max)
+            nc.vector.tensor_tensor(out=lo[:, t, cols], in0=pa[:, t, cols], in1=pb[:, t, cols], op=ALU.min)
+            nc.vector.tensor_tensor(out=pa[:, t, cols], in0=ya_win[t][:, cols], in1=hi[:, t, cols], op=ALU.min)
+            nc.vector.tensor_tensor(out=z_planes[:, t, cols], in0=pa[:, t, cols], in1=lo[:, t, cols], op=ALU.max)
+
+        for t in range(PACK - 1):
+            median(t, 0, S)
+        a_bank = [psum.tile([P, S], F32, name=f"bank{t}") for t in range(PACK)]
+        for c, (first, width) in enumerate(((0, HALF), (HALF, HALF))):
+            cols = slice(first, first + width)
+            median(PACK - 1, first, width)
             z_grouped = sb(f"z_grouped{c}", [P, width, PACK], BF16)
             z_w = sb(f"z_w{c}", [P, width], U32)
             z_sc = sb(f"z_sc{c}", [P, width], U8)
-            interleave(nc.vector.tensor_copy, z_grouped[:], pb[:])
+            interleave(nc.vector.tensor_copy, z_grouped[:], z_planes[:, :, cols])
             quantize(z_w[:], z_sc[:], z_grouped[:])
             for t in range(PACK):
                 product(a_bank[t][:, cols], cand_w[:, t, :], dealt_sc[:, 0, t, :], z_w[:], z_sc[:])
         for t in range(PACK):
-            nc.scalar.copy(out=b_win[t][:], in_=b_bank[t][:])
-        for t in range(PACK):
-            if t < 2:
-                nc.vector.tensor_scalar_mul(a_win[t][:], a_bank[t][:], 0.0625)
-            else:
-                nc.scalar.activation(out=a_win[t][:], in_=a_bank[t][:], func=COPY, scale=0.0625)
+            nc.scalar.copy(out=b_win[t][:, :S], in_=b_bank[t][:])
 
         out_rows = out_0.rearrange("(p t) n -> p t n", t=PACK)
         out_sc = sb("out_sc", [P, S], U8)
-        early = 2 * 2 * CHUNKS[0][1]
-        b_early = sb("b_early", [P, early], F32)
-        b_late = sb("b_late", [P, 2 * PACK * S - early], F32, tag=f"z_w{len(CHUNKS) - 1}")
-        b_near = {}
-        place = 0
-        for c, (first, width) in enumerate(CHUNKS):
-            for t in range(PACK):
-                for k, lst in enumerate((l_n5, l_n6)):
-                    if place < early:
-                        b_near[c, t, k] = b_early[:, place : place + width]
-                    else:
-                        b_near[c, t, k] = b_late[:, place - early : place - early + width]
-                    place += width
-                    nc.scalar.activation(out=b_near[c, t, k], in_=b_win[t][:].indirect(entries(lst, first, width)), func=COPY)
+        b_first = sb("b_first", [P, 2, S], F32)
+        b_rest = sb("b_rest", [P, PACK - 1, 2, S], F32, tag="z_w1")
+        sums = sb("sums", [P, PACK, 2, S], F32)
+        a_near = sb("a_near", [P, S], F32)
+        res = sb("res", [P, PACK, S], F32)
+
+        def fused_sum(t, k, lst, b_near, first, width):
+            cols = slice(first, first + width)
+            nc.vector.tensor_tensor(
+                out=sums[:, t, k, cols], in0=ya_win[t][:].indirect(entries(lst, first, width)), in1=b_near[:, k, cols], op=ALU.add
+            )
+
+        for t in range(PACK):
+            b_near = b_first[:] if t == 0 else b_rest[:, t - 1, :, :]
+            if t < 2:
+                nc.vector.tensor_scalar_mul(ya_win[t][:, :S], a_bank[t][:], 0.0625)
+            else:
+                nc.scalar.activation(out=ya_win[t][:, :S], in_=a_bank[t][:], func=COPY, scale=0.0625)
+            for k, lst in enumerate((l_n5, l_n6)):
+                nc.scalar.activation(out=b_near[:, k, :], in_=b_win[t][:].indirect(lst[:]), func=COPY)
+            if t < PACK - 1:
+                fused_sum(t, 0, l_n3, b_near, 0, S)
+                fused_sum(t, 1, l_n4, b_near, 0, S)
+                nc.vector.tensor_tensor(out=res[:, t, :], in0=sums[:, t, 0, :], in1=sums[:, t, 1, :], op=ALU.max)
+                nc.sync.dma_start(out_rows[:, t, :], res[:, t, :])
+        t = PACK - 1
+        for first in (0, HALF):
+            nc.scalar.activation(
+                out=a_near[:, first : first + HALF], in_=ya_win[t][:].indirect(entries(l_n4, first, HALF)), func=COPY
+            )
         for c, (first, width) in enumerate(CHUNKS):
             cols = slice(first, first + width)
-            sums = sb(f"sums{c}", [P, 2, PACK, width], F32)
-            res = sb(f"res{c}", [P, PACK, width], F32)
-            for t in range(PACK):
-                for k, lst in enumerate((l_n3, l_n4)):
-                    nc.vector.tensor_tensor(
-                        out=sums[:, k, t, :],
-                        in0=a_win[t][:].indirect(entries(lst, first, width)),
-                        in1=b_near[c, t, k],
-                        op=ALU.add,
-                    )
-            nc.vector.tensor_tensor(out=res[:], in0=sums[:, 0, :, :], in1=sums[:, 1, :, :], op=ALU.max)
-            nc.sync.dma_start(out_rows[:, :, cols], res[:])
+            fused_sum(t, 0, l_n3, b_near, first, width)
+            nc.vector.tensor_tensor(out=sums[:, t, 1, cols], in0=a_near[:, cols], in1=b_near[:, 1, cols], op=ALU.add)
+            nc.vector.tensor_tensor(out=res[:, t, cols], in0=sums[:, t, 0, cols], in1=sums[:, t, 1, cols], op=ALU.max)
+            nc.sync.dma_start(out_rows[:, t, cols], res[:, t, cols])
             res_grouped = sb(f"res_grouped{c}", [P, width, PACK], BF16)
-            interleave(nc.vector.tensor_copy if c == len(CHUNKS) - 1 else nc.scalar.copy, res_grouped[:], res[:])
+            interleave(nc.vector.tensor_copy if c == len(CHUNKS) - 1 else nc.scalar.copy, res_grouped[:], res[:, :, cols])
             out_w = sb(f"out_w{c}", [P, width], U32)
             quantize(out_w[:], out_sc[:, cols], res_grouped[:])
             nc.sync.dma_start(

@@ -73,6 +73,8 @@ def tile_picked_cdswpathbmed_none_po_kernel(
         b_win = [sb(f"b_win{t}", [P, 2 * S], F32) for t in range(PACK)]
         for win in ya_win[: PACK - 1] + b_win[:1]:
             nc.vector.memset(win[:, S:].bitcast(I32), 0)
+        for win in b_win[1:]:
+            nc.scalar.copy(out=win[:, S:], in_=b_win[0][:, S:])
 
         l_offs = load_list("l_offs", offs)
         for q in range(4):
@@ -86,8 +88,6 @@ def tile_picked_cdswpathbmed_none_po_kernel(
         load_scale_rows(nc.sync, w1_sc, w1_scales)
         gain = sb("gain", [P, PACK], F32)
         nc.gpsimd.dma_start(gain[:], gs.rearrange("(p t) o -> p (t o)", t=PACK))
-        for win in b_win[1:]:
-            nc.gpsimd.memset(win[:, S:].bitcast(I32), 0)
         l_cb = load_list("l_cb", cb)
         l_n1 = load_list("l_n1", n1)
         l_n2 = load_list("l_n2", n2)
@@ -110,7 +110,10 @@ def tile_picked_cdswpathbmed_none_po_kernel(
             cols = slice(h * HALF, (h + 1) * HALF)
             nc.vector.tensor_copy(out=q_w[h][:], in_=x_w[:].indirect(entries(l_offs, h * HALF, HALF)))
             if h == 0:
-                nc.vector.tensor_copy(out=w1_wd[:], in_=w1_w[:].rearrange("p (m t) -> p t m", t=PACK))
+                nc.vector.tensor_copy(
+                    out=w1_wd[:].rearrange("p t (c i) -> p c t i", i=4),
+                    in_=w1_w[:].rearrange("p (c i t) -> p c t i", i=4, t=PACK),
+                )
                 nc.vector.tensor_copy(out=w1_sd[:], in_=w1_sc[:].rearrange("p (m t) -> p t m", t=PACK))
             for u in range(2):
                 bank = psum.tile([P, 2, HALF], F32, name=f"bank{2 * h + u}")
@@ -167,13 +170,11 @@ def tile_picked_cdswpathbmed_none_po_kernel(
             quantize(z_w[:], z_sc[:], z_grouped[:])
             for t in range(PACK):
                 product(a_bank[t][:, cols], cand_w[:, t, :], dealt_sc[:, 0, t, :], z_w[:], z_sc[:])
-        for t in range(PACK):
-            nc.scalar.copy(out=b_win[t][:, :S], in_=b_bank[t][:])
 
         out_rows = out_0.rearrange("(p t) n -> p t n", t=PACK)
         out_sc = sb("out_sc", [P, S], U8)
-        b_first = sb("b_first", [P, 2, S], F32)
-        b_rest = sb("b_rest", [P, PACK - 1, 2, S], F32, tag="z_w1")
+        b_first = sb("b_first", [P, 2, 2, S], F32)
+        b_rest = sb("b_rest", [P, 2, 2, S], F32, tag="z_w1")
         sums = sb("sums", [P, PACK, 2, S], F32)
         a_near = sb("a_near", [P, S], F32)
         res = sb("res", [P, PACK, S], F32)
@@ -185,7 +186,8 @@ def tile_picked_cdswpathbmed_none_po_kernel(
             )
 
         for t in range(PACK):
-            b_near = b_first[:] if t == 0 else b_rest[:, t - 1, :, :]
+            b_near = b_first[:, t, :, :] if t < 2 else b_rest[:, t - 2, :, :]
+            nc.scalar.copy(out=b_win[t][:, :S], in_=b_bank[t][:])
             if t < 2:
                 nc.vector.tensor_scalar_mul(ya_win[t][:, :S], a_bank[t][:], 0.0625)
             else:

from contextlib import ExitStack

import concourse.mybir as mybir

F32 = mybir.dt.float32
BF16 = mybir.dt.bfloat16
I32 = mybir.dt.int32
U32 = mybir.dt.uint32
U16 = mybir.dt.uint16
U8 = mybir.dt.uint8
FP8X4 = mybir.dt.float8_e4m3fn_x4
ALU = mybir.AluOpType
COPY = mybir.ActivationFunctionType.Copy

P = 128
PACK = 4
T = 2048
S = 512
HALF = S // 2
CHUNKS = ((0, 256), (256, 128), (384, 128))

FLOPS = 3 * 2 * 512 * 512 * 512


def tile_picked_cdswpathbmed_none_po_kernel(
    tc, x_words, x_scales, w1_words, w1_scales, gs, wb, offs, n1, n2, cand, cb, n3, n4, n5, n6, out_0, out_1, out_2
):
    nc = tc.nc

    with ExitStack() as ctx:
        keep = ctx.enter_context(tc.tile_pool(name="keep", bufs=1))
        psum = ctx.enter_context(tc.psum_pool(name="psum", bufs=1))

        def sb(name, shape, dtype, tag=None):
            return keep.tile(shape, dtype, name=name, tag=tag or name, align_bytes=64)

        def load_list(name, src):
            t = keep.tile([P, S // 16], U16, name=name)
            nc.sync.dma_start(t[:], src)
            return t

        def entries(lst, first, count):
            return lst[:, first // 16 : (first + count) // 16]

        def load_scale_rows(queue, dst, src):
            for q in range(4):
                queue.dma_start(dst[32 * q : 32 * q + 4, :].bitcast(I32), src[0, 4 * q : 4 * q + 4, :].bitcast(I32))

        def words_view(src):
            return src[0].rearrange("p n t -> p (n t)")

        def interleave(move, dst, src):
            move(out=dst.rearrange("p (c i) t -> p c t i", i=4), in_=src.rearrange("p t (c i) -> p c t i", i=4))

        def quantize(codes, scales, grouped):
            nc.vector.quantize_mx(out=codes.bitcast(FP8X4), scales=scales, in_=grouped.rearrange("p n t -> p (n t)"))

        def product(dst, st_codes, st_scales, mv_codes, mv_scales):
            nc.tensor.matmul_mx(
                out=dst,
                lhsT=st_codes.bitcast(FP8X4),
                lhsT_scale=st_scales,
                rhs=mv_codes.bitcast(FP8X4),
                rhs_scale=mv_scales,
                start=True,
                stop=True,
            )

        x_sc = sb("x_sc", [P, T], U8)
        w1_sc = sb("w1_sc", [P, S], U8)
        nc.gpsimd.memset(w1_sc[:].bitcast(I32), 0)
        ya_win = [sb(f"ya_win{t}", [P, 2 * S if t < PACK - 1 else S], F32) for t in range(PACK)]
        b_win = [sb(f"b_win{t}", [P, 2 * S], F32) for t in range(PACK)]
        for win in ya_win[: PACK - 1] + b_win[:1]:
            nc.vector.memset(win[:, S:].bitcast(I32), 0)
        for win in b_win[1:]:
            nc.scalar.copy(out=win[:, S:], in_=b_win[0][:, S:])

        l_offs = load_list("l_offs", offs)
        for q in range(4):
            rows = x_scales[0, 4 * q : 4 * q + 4, :].bitcast(I32)
            nc.sync.dma_start(x_sc[32 * q : 32 * q + 32, :].bitcast(I32), rows.unsqueeze(0).broadcast_to([8, 4, T // 4]))
        l_cand = load_list("l_cand", cand)
        x_w = sb("x_w", [P, T], U32)
        nc.sync.dma_start(x_w[:].bitcast(I32), words_view(x_words).bitcast(I32))
        w1_w = sb("w1_w", [P, S], U32)
        nc.sync.dma_start(w1_w[:].bitcast(I32), words_view(w1_words).bitcast(I32))
        load_scale_rows(nc.sync, w1_sc, w1_scales)
        gain = sb("gain", [P, PACK], F32)
        nc.gpsimd.dma_start(gain[:], gs.rearrange("(p t) o -> p (t o)", t=PACK))
        l_cb = load_list("l_cb", cb)
        l_n1 = load_list("l_n1", n1)
        l_n2 = load_list("l_n2", n2)
        wb_raw = sb("wb_raw", [P, PACK, S], F32)
        nc.sync.dma_start(wb_raw[:], wb.rearrange("(p t) n -> p t n", t=PACK))
        l_n5 = load_list("l_n5", n5)
        l_n6 = load_list("l_n6", n6)
        l_n3 = load_list("l_n3", n3)
        l_n4 = load_list("l_n4", n4)

        q_sc = sb("q_sc", [P, S], U8)
        nc.vector.tensor_copy(out=q_sc[:], in_=x_sc[:].indirect(l_offs[:]))
        w1_wd = sb("w1_wd", [P, PACK, P], U32)
        picked_sc = sb("picked_sc", [P, 2, S], U8)
        nc.vector.tensor_copy(out=picked_sc[:, 0, :], in_=x_sc[:].indirect(l_cand[:]))
        w1_sd = sb("w1_sd", [P, PACK, P], U8)

        q_w = [sb("q_w0", [P, HALF], U32), sb("q_w1", [P, HALF], U32, tag="w1_sc")]
        for h in range(2):
            cols = slice(h * HALF, (h + 1) * HALF)
            nc.vector.tensor_copy(out=q_w[h][:], in_=x_w[:].indirect(entries(l_offs, h * HALF, HALF)))
            if h == 0:
                nc.vector.tensor_copy(
                    out=w1_wd[:].rearrange("p t (c i) -> p c t i", i=4),
                    in_=w1_w[:].rearrange("p (c i t) -> p c t i", i=4, t=PACK),
                )
                nc.vector.tensor_copy(out=w1_sd[:], in_=w1_sc[:].rearrange("p (m t) -> p t m", t=PACK))
            for u in range(2):
                bank = psum.tile([P, 2, HALF], F32, name=f"bank{2 * h + u}")
                for e in range(2):
                    t = 2 * u + e
                    product(bank[:, e, :], w1_wd[:, t, :], w1_sd[:, t, :], q_w[h][:], q_sc[:, cols])
                for e in range(2):
                    t = 2 * u + e
                    nc.scalar.activation(out=ya_win[t][:, cols], in_=bank[:, e, :], func=COPY, scale=gain[:, t : t + 1])

        cb_w = sb("cb_w", [P, PACK, P], U32)
        nc.vector.tensor_copy(out=picked_sc[:, 1, :], in_=x_sc[:].indirect(l_cb[:]))
        nc.vector.tensor_copy(out=cb_w[:].rearrange("p t m -> p m t"), in_=x_w[:].indirect(l_cb[:]))
        dealt_sc = sb("dealt_sc", [P, 2, PACK, P], U8)
        nc.vector.tensor_copy(out=dealt_sc[:], in_=picked_sc[:].rearrange("p l (m t) -> p l t m", t=PACK))

        cand_w = sb("cand_w", [P, PACK, P], U32, tag="w1_sc")
        nc.vector.tensor_copy(out=cand_w[:].rearrange("p t m -> p m t"), in_=x_w[:].indirect(l_cand[:]))
        wb_grouped = sb("wb_grouped", [P, S, PACK], BF16)
        interleave(nc.vector.tensor_copy, wb_grouped[:], wb_raw[:])

        wb_w = sb("wb_w", [P, S], U32)
        wb_sc = sb("wb_sc", [P, S], U8)
        quantize(wb_w[:], wb_sc[:], wb_grouped[:])
        b_bank = [psum.tile([P, S], F32, name=f"bank{4 + t}") for t in range(PACK)]
        for t in range(PACK):
            product(b_bank[t][:], cb_w[:, t, :], dealt_sc[:, 1, t, :], wb_w[:], wb_sc[:])

        pa = sb("pa", [P, PACK, S], BF16)
        pb = sb("pb", [P, PACK, S], BF16)
        lo = sb("lo", [P, PACK, S], BF16)
        hi = sb("hi", [P, PACK, S], BF16)
        z_planes = sb("z_planes", [P, PACK, S], BF16)

        def median(t, first, width):
            cols = slice(first, first + width)
            nc.scalar.activation(out=pa[:, t, cols], in_=ya_win[t][:].indirect(entries(l_n1, first, width)), func=COPY)
            nc.scalar.activation(out=pb[:, t, cols], in_=ya_win[t][:].indirect(entries(l_n2, first, width)), func=COPY)
            nc.vector.tensor_tensor(out=hi[:, t, cols], in0=pa[:, t, cols], in1=pb[:, t, cols], op=ALU.max)
            nc.vector.tensor_tensor(out=lo[:, t, cols], in0=pa[:, t, cols], in1=pb[:, t, cols], op=ALU.min)
            nc.vector.tensor_tensor(out=pa[:, t, cols], in0=ya_win[t][:, cols], in1=hi[:, t, cols], op=ALU.min)
            nc.vector.tensor_tensor(out=z_planes[:, t, cols], in0=pa[:, t, cols], in1=lo[:, t, cols], op=ALU.max)

        for t in range(PACK - 1):
            median(t, 0, S)
        a_bank = [psum.tile([P, S], F32, name=f"bank{t}") for t in range(PACK)]
        for c, (first, width) in enumerate(((0, HALF), (HALF, HALF))):
            cols = slice(first, first + width)
            median(PACK - 1, first, width)
            z_grouped = sb(f"z_grouped{c}", [P, width, PACK], BF16)
            z_w = sb(f"z_w{c}", [P, width], U32)
            z_sc = sb(f"z_sc{c}", [P, width], U8)
            interleave(nc.vector.tensor_copy, z_grouped[:], z_planes[:, :, cols])
            quantize(z_w[:], z_sc[:], z_grouped[:])
            for t in range(PACK):
                product(a_bank[t][:, cols], cand_w[:, t, :], dealt_sc[:, 0, t, :], z_w[:], z_sc[:])

        out_rows = out_0.rearrange("(p t) n -> p t n", t=PACK)
        out_sc = sb("out_sc", [P, S], U8)
        b_first = sb("b_first", [P, 2, 2, S], F32)
        b_rest = sb("b_rest", [P, 2, 2, S], F32, tag="z_w1")
        sums = sb("sums", [P, PACK, 2, S], F32)
        a_near = sb("a_near", [P, S], F32)
        res = sb("res", [P, PACK, S], F32)

        def fused_sum(t, k, lst, b_near, first, width):
            cols = slice(first, first + width)
            nc.vector.tensor_tensor(
                out=sums[:, t, k, cols], in0=ya_win[t][:].indirect(entries(lst, first, width)), in1=b_near[:, k, cols], op=ALU.add
            )

        for t in range(PACK):
            b_near = b_first[:, t, :, :] if t < 2 else b_rest[:, t - 2, :, :]
            nc.scalar.copy(out=b_win[t][:, :S], in_=b_bank[t][:])
            if t < 2:
                nc.vector.tensor_scalar_mul(ya_win[t][:, :S], a_bank[t][:], 0.0625)
            else:
                nc.scalar.activation(out=ya_win[t][:, :S], in_=a_bank[t][:], func=COPY, scale=0.0625)
            for k, lst in enumerate((l_n5, l_n6)):
                nc.scalar.activation(out=b_near[:, k, :], in_=b_win[t][:].indirect(lst[:]), func=COPY)
            if t < PACK - 1:
                fused_sum(t, 0, l_n3, b_near, 0, S)
                fused_sum(t, 1, l_n4, b_near, 0, S)
                nc.vector.tensor_tensor(out=res[:, t, :], in0=sums[:, t, 0, :], in1=sums[:, t, 1, :], op=ALU.max)
                nc.sync.dma_start(out_rows[:, t, :], res[:, t, :])
        t = PACK - 1
        for first in (0, HALF):
            nc.scalar.activation(
                out=a_near[:, first : first + HALF], in_=ya_win[t][:].indirect(entries(l_n4, first, HALF)), func=COPY
            )
        for c, (first, width) in enumerate(CHUNKS):
            cols = slice(first, first + width)
            fused_sum(t, 0, l_n3, b_near, first, width)
            nc.vector.tensor_tensor(out=sums[:, t, 1, cols], in0=a_near[:, cols], in1=b_near[:, 1, cols], op=ALU.add)
            nc.vector.tensor_tensor(out=res[:, t, cols], in0=sums[:, t, 0, cols], in1=sums[:, t, 1, cols], op=ALU.max)
            nc.sync.dma_start(out_rows[:, t, cols], res[:, t, cols])
            res_grouped = sb(f"res_grouped{c}", [P, width, PACK], BF16)
            interleave(nc.vector.tensor_copy if c == len(CHUNKS) - 1 else nc.scalar.copy, res_grouped[:], res[:, :, cols])
            out_w = sb(f"out_w{c}", [P, width], U32)
            quantize(out_w[:], out_sc[:, cols], res_grouped[:])
            nc.sync.dma_start(
                words_view(out_1)[:, PACK * first : PACK * (first + width)].bitcast(I32), out_w[:].bitcast(I32)
            )
        for q in range(4):
            queue = nc.sync if q % 2 else nc.scalar
            queue.dma_start(out_2[0, 4 * q : 4 * q + 4, :].bitcast(I32), out_sc[32 * q : 32 * q + 4, :].bitcast(I32))
